import numpy as np
import ml_dtypes

BF16 = ml_dtypes.bfloat16


def bf(x):
    return np.asarray(x, np.float32).astype(BF16)


def f32(x):
    return np.asarray(x, np.float32)


def f64(x):
    return np.asarray(x).astype(np.float64)


def striped(idx):
    return np.tile(idx.reshape(-1, 16).T, (8, 1))


S, A, K, M, N, E, Q = 512, 128, 256, 128, 192, 1, 192


def setup_inputs():
    return {"x": bf(np.random.standard_normal((A, S))), "wd": bf(np.random.standard_normal((A, M)) / np.sqrt(A)), "y": bf(np.random.standard_normal((K, N))), "w": bf(np.random.standard_normal((K, M)) / np.sqrt(K)), "b": f32(0.5 * np.random.standard_normal((M, 1))), "offs": striped(np.random.permutation(S)[:N])}


def reference(x, wd, y, w, b, offs):
    idx = offs[:16].T.reshape(-1)
    z = f64(wd).T @ f64(x)
    z[:, idx] += f64(w).T @ f64(y)
    return z + f64(b)

@@ -1,0 +1,45 @@
+import concourse.mybir as mybir
+
+BF16, F32, U16 = mybir.dt.bfloat16, mybir.dt.float32, mybir.dt.uint16
+
+P = 128
+S = 512
+N = 192
+K_BLOCKS = 2
+FLOPS = 2 * P * P * S + 2 * K_BLOCKS * P * P * N
+
+
+def tile_rows_fillproj_bias_kernel(tc, x, wd, y, w, b, offs, out):
+    nc = tc.nc
+    with (
+        tc.tile_pool(name="held", bufs=1) as held,
+        tc.psum_pool(name="psum", bufs=1) as psum,
+    ):
+        x_tile = held.tile([P, S], BF16)
+        wd_tile = held.tile([P, P], BF16)
+        w_tile = held.tile([P, K_BLOCKS * P], BF16)
+        y_tile = held.tile([P, K_BLOCKS * N], BF16)
+        offsets = held.tile([P, N // 16], U16)
+        bias = held.tile([P, 1], F32)
+
+        nc.sync.dma_start(wd_tile[:], wd)
+        nc.sync.dma_start(x_tile[:], x)
+        nc.sync.dma_start(w_tile[:], w.rearrange("(p a) m -> p (a m)", a=K_BLOCKS))
+        nc.sync.dma_start(y_tile[:], y.rearrange("(p a) n -> p (a n)", a=K_BLOCKS))
+        nc.sync.dma_start(offsets[:], offs)
+        nc.sync.dma_start(bias[:], b)
+
+        z = psum.tile([P, S], F32)
+        nc.tensor.matmul(z[:], wd_tile[:], x_tile[:], start=True, stop=False)
+        for a in range(K_BLOCKS):
+            nc.tensor.matmul(
+                z[:].indirect(offsets[:]),
+                w_tile[:, a * P : (a + 1) * P],
+                y_tile[:, a * N : (a + 1) * N],
+                start=False,
+                stop=a == K_BLOCKS - 1,
+            )
+
+        result = held.tile([P, S], F32)
+        nc.vector.tensor_scalar_add(result[:], z[:], bias[:, 0:1])
+        nc.sync.dma_start(out, result[:])

@@ -6,6 +6,7 @@ P = 128
 S = 512
 N = 192
 K_BLOCKS = 2
+WARM_UPS = 4
 FLOPS = 2 * P * P * S + 2 * K_BLOCKS * P * P * N
 
 
@@ -21,6 +22,12 @@ def tile_rows_fillproj_bias_kernel(tc, x, wd, y, w, b, offs, out):
         y_tile = held.tile([P, K_BLOCKS * N], BF16)
         offsets = held.tile([P, N // 16], U16)
         bias = held.tile([P, 1], F32)
+
+        zeros = held.tile([P, S], BF16)
+        nc.vector.memset(zeros[:], 0.0)
+        spare = psum.tile([P, S], F32)
+        for i in range(WARM_UPS):
+            nc.tensor.matmul(spare[:], zeros[:, 0:P], zeros[:], start=True, stop=True)
 
         nc.sync.dma_start(wd_tile[:], wd)
         nc.sync.dma_start(x_tile[:], x)

@@ -6,7 +6,7 @@ P = 128
 S = 512
 N = 192
 K_BLOCKS = 2
-WARM_UPS = 4
+WARM_UPS = 6
 FLOPS = 2 * P * P * S + 2 * K_BLOCKS * P * P * N
 
 
@@ -23,9 +23,9 @@ def tile_rows_fillproj_bias_kernel(tc, x, wd, y, w, b, offs, out):
         offsets = held.tile([P, N // 16], U16)
         bias = held.tile([P, 1], F32)
 
-        zeros = held.tile([P, S], BF16)
+        zeros = held.tile([P, S // 2], BF16)
         nc.vector.memset(zeros[:], 0.0)
-        spare = psum.tile([P, S], F32)
+        spare = psum.tile([P, S // 2], F32)
         for i in range(WARM_UPS):
             nc.tensor.matmul(spare[:], zeros[:, 0:P], zeros[:], start=True, stop=True)
 
@@ -47,6 +47,8 @@ def tile_rows_fillproj_bias_kernel(tc, x, wd, y, w, b, offs, out):
                 stop=a == K_BLOCKS - 1,
             )
 
-        result = held.tile([P, S], F32)
-        nc.vector.tensor_scalar_add(result[:], z[:], bias[:, 0:1])
-        nc.sync.dma_start(out, result[:])
+        for h in range(2):
+            half = slice(h * (S // 2), (h + 1) * (S // 2))
+            result = held.tile([P, S // 2], F32, name=f"result{h}")
+            nc.vector.tensor_scalar_add(result[:], z[:, half], bias[:, 0:1])
+            nc.sync.dma_start(out[:, half], result[:])

import concourse.mybir as mybir

BF16, F32, U16 = mybir.dt.bfloat16, mybir.dt.float32, mybir.dt.uint16

P = 128
S = 512
N = 192
K_BLOCKS = 2
WARM_UPS = 6
FLOPS = 2 * P * P * S + 2 * K_BLOCKS * P * P * N


def tile_rows_fillproj_bias_kernel(tc, x, wd, y, w, b, offs, out):
    nc = tc.nc
    with (
        tc.tile_pool(name="held", bufs=1) as held,
        tc.psum_pool(name="psum", bufs=1) as psum,
    ):
        x_tile = held.tile([P, S], BF16)
        wd_tile = held.tile([P, P], BF16)
        w_tile = held.tile([P, K_BLOCKS * P], BF16)
        y_tile = held.tile([P, K_BLOCKS * N], BF16)
        offsets = held.tile([P, N // 16], U16)
        bias = held.tile([P, 1], F32)

        zeros = held.tile([P, S // 2], BF16)
        nc.vector.memset(zeros[:], 0.0)
        spare = psum.tile([P, S // 2], F32)
        for i in range(WARM_UPS):
            nc.tensor.matmul(spare[:], zeros[:, 0:P], zeros[:], start=True, stop=True)

        nc.sync.dma_start(wd_tile[:], wd)
        nc.sync.dma_start(x_tile[:], x)
        nc.sync.dma_start(w_tile[:], w.rearrange("(p a) m -> p (a m)", a=K_BLOCKS))
        nc.sync.dma_start(y_tile[:], y.rearrange("(p a) n -> p (a n)", a=K_BLOCKS))
        nc.sync.dma_start(offsets[:], offs)
        nc.sync.dma_start(bias[:], b)

        z = psum.tile([P, S], F32)
        nc.tensor.matmul(z[:], wd_tile[:], x_tile[:], start=True, stop=False)
        for a in range(K_BLOCKS):
            nc.tensor.matmul(
                z[:].indirect(offsets[:]),
                w_tile[:, a * P : (a + 1) * P],
                y_tile[:, a * N : (a + 1) * N],
                start=False,
                stop=a == K_BLOCKS - 1,
            )

        for h in range(2):
            half = slice(h * (S // 2), (h + 1) * (S // 2))
            result = held.tile([P, S // 2], F32, name=f"result{h}")
            nc.vector.tensor_scalar_add(result[:], z[:, half], bias[:, 0:1])
            nc.sync.dma_start(out[:, half], result[:])
